import numpy as np, ml_dtypes
CORES = [3,11,19,27,35,43,51,59]
N = 8
import mx_ref
BF = ml_dtypes.bfloat16
def entries(a):
    return np.ascontiguousarray(a.T).reshape(-1)
def table(e):
    return np.ascontiguousarray(np.reshape(e, (-1, 16)).T).astype(np.int32)
def cut(t, i, w=512):
    return t[:, w * i:w * i + w]
def decode(q):
    o = []
    for b in range(4):
        e = np.zeros((128, 128, 4), np.float32); e[np.arange(128), np.arange(128), b] = 1
        o.append(mx_ref.matmul(mx_ref.quantize(e.reshape(128, 512).astype(BF)), q))
    return np.stack(o, axis=2).reshape(128, -1)
def f(rng, *shape):
    return mx_ref.flush((rng.standard_normal(shape, dtype=np.float32) * np.exp2(rng.integers(-2, 3, shape[:-1] + (1,)))).astype(BF))
def wide(rng, *shape, cols=0):
    v = rng.standard_normal(shape, dtype=np.float32) * np.exp2(rng.integers(-12, 13, shape)).astype(np.float32)
    if cols: v *= np.repeat(np.exp2(rng.integers(-cols, cols + 1, shape[:-2] + (1, shape[-1] // 4))) * (rng.random(shape[:-2] + (1, shape[-1] // 4)) > 0.0625), 4, axis=-1).astype(np.float32)
    return mx_ref.flush(v.astype(BF))
T, K, O = 256, 256, 2
HA = (1237, 1811, 947, 1543, 2017, 733, 1409, 1699)
HB = (40503, 12289, 58111, 3571, 27644, 61007, 19211, 50021)
def setup_inputs(rng):
    return {"tb": f(rng, N, 128, 4 * K), "ids": np.stack([table(rng.integers(0, 4096, T)) for r in range(N)]), "w": f(rng, N, 128, 512 * O)}
def setup_inputs_alike(rng):
    d = setup_inputs(rng); e = rng.integers(0, 4096, T)
    d["ids"] = np.stack([table(e) for r in range(N)]); return d
def setup_inputs_ends(rng):
    d = setup_inputs(rng); o = []
    for r in range(N):
        e = rng.choice([0, 4095], T); e[rng.permutation(T)[:2]] = [0, 4095]
        o.append(table(e))
    d["ids"] = np.stack(o); return d
def setup_inputs_order(rng):
    d = setup_inputs(rng); t = rng.standard_normal((N, 128, 4 * K), dtype=np.float32)
    one = rng.permutation(np.concatenate([np.arange(N), rng.integers(0, N, 16 - N)]))
    for g in range(16):
        p = int(one[g]); o = int(rng.choice([q for q in range(N) if abs(q - p) >= 2]))
        size = np.float32(2.0 ** int(rng.integers(0, 3)))
        X = np.tile(rng.choice([-1, 1], (8, 4)).astype(np.float32) * size, (1, K))
        v = t[:, 8 * g:8 * g + 8]; v *= size * np.float32(2.0 ** -14)
        v[min(p, o)] = X; v[max(p, o)] = -X
    d["tb"] = mx_ref.flush(t.astype(BF)); return d
def setup_inputs_same(rng):
    d = setup_inputs(rng)
    d["ids"] = np.stack([table(np.full(T, rng.integers(0, 4096))) for r in range(N)]); return d
def setup_inputs_spread(rng):
    d = setup_inputs(rng); d["tb"] = wide(rng, N, 128, 4 * K, cols=8); return d
def check_inputs(d):
    b = []
    for r in range(N):
        e = entries(d["ids"][r])
        if e.min() < 0 or e.max() > 4095: b.append("ids")
    return b
def address(q, e):
    return ((e * HA[q] + HB[q]) >> 5) & (K - 1)
def reference(tb, ids, w):
    d = [decode(mx_ref.quantize(tb[q])).reshape(128, -1, 4) for q in range(N)]
    y = np.zeros((N, 128, O * T), np.float32)
    for r in range(N):
        e = entries(ids[r])
        v = d[0][:, address(0, e)]
        for q in range(1, N): v = v + d[q][:, address(q, e)]
        V = mx_ref.quantize(np.ascontiguousarray(v.reshape(128, -1)).astype(BF))
        for o in range(O): y[r][:, T * o:T * o + T] = mx_ref.matmul(mx_ref.quantize(np.ascontiguousarray(cut(w[r], o))), V)
    return {"y": y}

@@ -1,0 +1,233 @@
+from concourse.bass import DstId, RemoteDMATransfer
+from concourse.mybir import dt, AluOpType, ActivationFunctionType
+
+N, TOK, K, O = 8, 256, 256, 2
+HA = (1237, 1811, 947, 1543, 2017, 733, 1409, 1699)
+HB = (40503, 12289, 58111, 3571, 27644, 61007, 19211, 50021)
+LW = 16 * (N - 1)
+
+SCRATCH = {
+    "ids8": ("sbuf", [128, 16], "int32"),
+    "ox": ("sbuf", [128, 16], "int32"),
+    "oy": ("sbuf", [128, 16], "int32"),
+    "oo": ("sbuf", [128, 64], "uint16"),
+    "lst": ("sbuf", [128, LW], "int32"),
+    "lx": ("sbuf", [128, LW], "int32"),
+    "ly": ("sbuf", [128, LW], "int32"),
+    "lo": ("sbuf", [128, 4 * LW], "uint16"),
+    "tbs": ("sbuf", [128, 4 * K], "bfloat16"),
+    "ws": ("sbuf", [128, 512 * O], "bfloat16"),
+    "ones": ("sbuf", [128, 520], "bfloat16"),
+    "ez": ("sbuf", [128, 520], "bfloat16"),
+    "ec": ("sbuf", [128, 512], "float8_e4m3fn_x4"),
+    "es": ("sbuf", [128, 512], "uint8"),
+    "wc": ("sbuf", [128, 128 * O], "float8_e4m3fn_x4"),
+    "wp": ("sbuf", [128, 128 * O], "uint8"),
+    "rc": ("sbuf", [128, N * TOK], "float8_e4m3fn_x4"),
+    "rs": ("sbuf", [128, N * TOK], "uint8"),
+    "hc": ("sbuf", [128, TOK], "float8_e4m3fn_x4"),
+    "hs": ("sbuf", [128, TOK], "uint8"),
+    "vt": ("sbuf", [128, 4 * TOK], "bfloat16"),
+    "vc": ("sbuf", [128, TOK], "float8_e4m3fn_x4"),
+    "vs": ("sbuf", [128, TOK], "uint8"),
+    "yo": ("sbuf", [128, O * TOK], "float32"),
+    "ps": ("psum", [128, 512 * 6], "float32"),
+}
+for _i in range(N):
+    SCRATCH["h%d" % _i] = ("sbuf", [128, 4 * TOK], "bfloat16")
+for _i in range(N - 1):
+    SCRATCH["qc%d" % _i] = ("sbuf", [128, TOK], "float8_e4m3fn_x4")
+    SCRATCH["qs%d" % _i] = ("sbuf", [128, TOK], "uint8")
+
+SEMAPHORES = ["idl", "tbl", "wl", "v", "s", "t", "ga", "lists", "sent", "hcode", "hplane", "yd"] + ["arr%d" % q for q in range(N)]
+
+
+def bits(m):
+    return bin(m).count("1")
+
+
+def plan(core, T, topo):
+    ch = topo.chip(core)
+    r = T.rank_of(core)
+    ring = [(r + k) % N for k in range(1, N)]
+    mate = [d for d in ring if topo.mates(ch, topo.chip(T.cores[d]))]
+    plane = [d for d in ring if topo.same_plane(ch, topo.chip(T.cores[d]))]
+    far = [d for d in ring if d not in mate and d not in plane]
+    help_ = [c for c in topo.cores_of(core) if c != core and all(topo.may_write(c, T.cores[d]) for d in far)]
+    help_.sort(key=lambda c: (topo.die(c) == topo.die(core), c))
+    relayed = [(d, help_[i]) for i, d in enumerate(far)]
+    direct = [(d, None) for d in plane[:2] + mate + plane[2:]]
+    return relayed[:2] + direct[:1] + relayed[2:] + direct[1:]
+
+
+def rank_program(g, core, T, topo):
+    rank = T.rank_of(core)
+    if rank is None:
+        helper_program(g, core, T, topo)
+        return
+    owner_program(g, core, rank, T, topo)
+
+
+def helper_program(g, core, T, topo):
+    for src in T.cores:
+        if topo.chip(src) != topo.chip(core):
+            continue
+        for d, h in plan(src, T, topo):
+            if h != core:
+                continue
+            q = T.rank_of(src)
+            dst = T.cores[d]
+            rid, pid, _ = topo.addr(dst)
+            n_in = bits(local_mask(src, core, T, topo))
+            m = topo.mask(core, dst)
+            arr = T.sem["arr%d" % q]
+            g.wait_ge(T.sem.hcode, n_in)
+            g.remote_dma(T.rc[:, TOK * q:TOK * q + TOK].bitcast(dt.uint8), T.hc[:, 0:TOK].bitcast(dt.uint8), arr, T.sem.sent, pid, rid, m)
+            g.wait_ge(T.sem.hplane, n_in)
+            g.remote_dma(T.rs[:, TOK * q:TOK * q + TOK], T.hs[:, 0:TOK], arr, T.sem.sent, pid, rid, m)
+            g.wait_ge(T.sem.sent, 2 * bits(m))
+
+
+def local_mask(src, helper, T, topo):
+    off = 0
+    for c in T.cores:
+        if topo.chip(c) != topo.chip(src):
+            off |= topo.mask(src, c)
+    return topo.mask(src, helper) & ~off
+
+
+def owner_program(g, core, r, T, topo):
+    vec, sca, ten, syn = g.vector, g.scalar, g.tensor, g.sync
+    A = AluOpType
+    COPY = ActivationFunctionType.Copy
+    cnt = {"v": 0, "s": 0, "t": 0}
+    seen = {}
+
+    def done(name, ins):
+        ins.then_inc(T.sem[name], 1)
+        cnt[name] += 1
+        return cnt[name]
+
+    def need(queue, me, name, val):
+        if val > seen.get((me, name), 0):
+            queue.wait_ge(T.sem[name], val)
+            seen[(me, name)] = val
+
+    order = plan(core, T, topo)
+    others = [d for d in range(N) if d != r]
+
+    for i in range(8):
+        (syn if i < 4 else sca).dma_start(T.ids8[16 * i:16 * i + 16, :], T.ids[:, :]).then_inc(T.sem.idl, 16)
+    syn.dma_start(T.tbs[:, :], T.tb[:, :]).then_inc(T.sem.tbl, 16)
+    sca.dma_start(T.ws[:, :], T.w[:, :]).then_inc(T.sem.wl, 16)
+
+    n_ones = done("v", vec.memset(T.ones[:, :], 1.0))
+    g.wait_ge(T.sem.v, n_ones)
+    g.affine_select(T.ez[:, :], T.ones[:, :], [[1, 520]], A.is_equal, 0.0, -4, -4).then_inc(T.sem.ga, 1)
+
+    g.wait_ge(T.sem.idl, 128)
+    ids_, dsts, mask = [], [], None
+    for d in others:
+        dst = T.cores[d]
+        rid, pid, _ = topo.addr(dst)
+        slot = r if r < d else r - 1
+        ids_.append(DstId(rid=rid, pnc=pid))
+        dsts.append(T.lst[:, 16 * slot:16 * slot + 16])
+        m = topo.mask(core, dst)
+        mask = m if mask is None else mask & m
+    sent = bits(mask)
+    g.remote_dma_fused([RemoteDMATransfer(dst_ids=ids_, dma_engine_mask=mask, remote_sem=T.sem.lists, srcs=[T.ids8[:, :]], dsts=dsts)], local_sem=T.sem.sent)
+
+    vec.wait_ge(T.sem.ga, 1)
+    for b in range(4):
+        n_e = done("v", vec.quantize_mx(T.ec[:, 128 * b:128 * b + 128], T.es[:, 128 * b:128 * b + 128], T.ez[:, 4 - b:4 - b + 512]))
+
+    def hashes(src, x, y, off, w):
+        n = done("v", vec.tensor_scalar(x[:, :], src[:, :], HA[r], HB[r], A.mult, A.add))
+        need(vec, "v", "v", n)
+        n = done("v", vec.tensor_scalar(y[:, :], x[:, :], 3, 4 * (K - 1), A.arith_shift_right, A.bitwise_and))
+        need(vec, "v", "v", n)
+        return [done("v", vec.tensor_scalar(off[:, w * t:w * t + w], y[:, :], t, None, A.add)) for t in range(4)]
+
+    def gather(h, off, w, c, ns, outs, n_off):
+        win = T.tbs[:, 0:4 * K]
+        for t in range(4):
+            o = win.indirect(off[:, w * t + c:w * t + c + 16])
+            if t < ns:
+                need(sca, "s", "v", n_off[t])
+                n_s = done("s", sca.activation(h[:, t:4 * TOK:4], o, COPY))
+            else:
+                need(vec, "v", "v", n_off[t])
+                n_v = done("v", vec.tensor_copy(h[:, t:4 * TOK:4], o))
+        need(vec, "v", "v", n_v)
+        need(vec, "v", "s", n_s)
+        return done("v", vec.quantize_mx(outs[0], outs[1], h[:, 0:4 * TOK]))
+
+    vec.wait_ge(T.sem.idl, 128)
+    n_off = hashes(T.ids8, T.ox, T.oy, T.oo, 16)
+    vec.wait_ge(T.sem.tbl, 16)
+    sca.wait_ge(T.sem.tbl, 16)
+    n_own = gather(T["h%d" % (N - 1)], T.oo, 16, 0, 2,
+                   (T.rc[:, TOK * r:TOK * r + TOK], T.rs[:, TOK * r:TOK * r + TOK]), n_off)
+
+    vec.wait_ge(T.sem.lists, sent * (N - 1))
+    n_off = hashes(T.lst, T.lx, T.ly, T.lo, LW)
+    for i, (d, helper) in enumerate(order):
+        qc, qs = T["qc%d" % i], T["qs%d" % i]
+        slot = d if d < r else d - 1
+        n_q = gather(T["h%d" % i], T.lo, LW, 16 * slot, 3 if i == len(order) - 1 else 2, (qc[:, 0:TOK], qs[:, 0:TOK]), n_off)
+        g.wait_ge(T.sem.v, n_q)
+        if helper is None:
+            dst = T.cores[d]
+            oc, op = T.rc[:, TOK * r:TOK * r + TOK], T.rs[:, TOK * r:TOK * r + TOK]
+            sc = sp = T.sem["arr%d" % r]
+            m = topo.mask(core, dst)
+        else:
+            dst = helper
+            oc, op = T.hc[:, 0:TOK], T.hs[:, 0:TOK]
+            sc, sp = T.sem.hcode, T.sem.hplane
+            m = local_mask(core, helper, T, topo)
+        rid, pid, _ = topo.addr(dst)
+        g.remote_dma(oc.bitcast(dt.uint8), qc[:, 0:TOK].bitcast(dt.uint8), sc, T.sem.sent, pid, rid, m)
+        g.remote_dma(op, qs[:, 0:TOK], sp, T.sem.sent, pid, rid, m)
+        sent += 2 * bits(m)
+
+    vec.wait_ge(T.sem.wl, 16)
+    n_w = done("v", vec.quantize_mx(T.wc[:, 0:128 * O], T.wp[:, 0:128 * O], T.ws[:, 0:512 * O]))
+
+    need(ten, "t", "v", n_e)
+    n_t = [0] * 4
+    for q in range(N):
+        if q == r:
+            need(ten, "t", "v", n_own)
+        else:
+            ten.wait_ge(T.sem["arr%d" % q], 2 * bits(mask))
+        for b in range(4):
+            n_t[b] = done("t", ten.matmul_mx(T.ps[:, 512 * b:512 * b + TOK], T.ec[:, 128 * b:128 * b + 128], T.es[:, 128 * b:128 * b + 128],
+                                             T.rc[:, TOK * q:TOK * q + TOK], T.rs[:, TOK * q:TOK * q + TOK], q == 0, q == N - 1))
+
+    for b in range(4):
+        o, i = T.vt[:, b:4 * TOK:4], T.ps[:, 512 * b:512 * b + TOK]
+        if b % 2 == 0:
+            need(sca, "s", "t", n_t[b])
+            n_s = done("s", sca.activation(o, i, COPY))
+        else:
+            need(vec, "v", "t", n_t[b])
+            n_v = done("v", vec.tensor_copy(o, i))
+    need(vec, "v", "v", n_v)
+    need(vec, "v", "s", n_s)
+    n_q = done("v", vec.quantize_mx(T.vc[:, 0:TOK], T.vs[:, 0:TOK], T.vt[:, 0:4 * TOK]))
+    need(ten, "t", "v", n_w)
+    need(ten, "t", "v", n_q)
+    n_y = [done("t", ten.matmul_mx(T.ps[:, 512 * (4 + o):512 * (4 + o) + TOK], T.wc[:, 128 * o:128 * o + 128], T.wp[:, 128 * o:128 * o + 128],
+                                   T.vc[:, 0:TOK], T.vs[:, 0:TOK], True, True)) for o in range(O)]
+    need(sca, "s", "t", n_y[0])
+    n_s = done("s", sca.activation(T.yo[:, 0:TOK], T.ps[:, 2048:2048 + TOK], COPY))
+    need(sca, "s", "s", n_s)
+    sca.dma_start(T.y[:, 0:TOK], T.yo[:, 0:TOK]).then_inc(T.sem.yd, 16)
+    need(vec, "v", "t", n_y[1])
+    n_v = done("v", vec.tensor_copy(T.yo[:, TOK:2 * TOK], T.ps[:, 2560:2560 + TOK]))
+    need(syn, "y", "v", n_v)
+    syn.dma_start(T.y[:, TOK:2 * TOK], T.yo[:, TOK:2 * TOK]).then_inc(T.sem.yd, 16)
+    syn.wait_ge(T.sem.yd, 32)
+    g.wait_ge(T.sem.sent, sent)

@@ -4,18 +4,20 @@ from concourse.mybir import dt, AluOpType, ActivationFunctionType
 N, TOK, K, O = 8, 256, 256, 2
 HA = (1237, 1811, 947, 1543, 2017, 733, 1409, 1699)
 HB = (40503, 12289, 58111, 3571, 27644, 61007, 19211, 50021)
+EARLY = 3
+SHARE = (2, 2, 3, 2, 2, 3, 2)
 LW = 16 * (N - 1)
+WIN = 4 * K - 3
 
 SCRATCH = {
     "ids8": ("sbuf", [128, 16], "int32"),
     "ox": ("sbuf", [128, 16], "int32"),
     "oy": ("sbuf", [128, 16], "int32"),
-    "oo": ("sbuf", [128, 64], "uint16"),
+    "oo": ("sbuf", [128, 16], "uint16"),
     "lst": ("sbuf", [128, LW], "int32"),
     "lx": ("sbuf", [128, LW], "int32"),
     "ly": ("sbuf", [128, LW], "int32"),
-    "lo": ("sbuf", [128, 4 * LW], "uint16"),
-    "tbs": ("sbuf", [128, 4 * K], "bfloat16"),
+    "lo": ("sbuf", [128, LW], "uint16"),
     "ws": ("sbuf", [128, 512 * O], "bfloat16"),
     "ones": ("sbuf", [128, 520], "bfloat16"),
     "ez": ("sbuf", [128, 520], "bfloat16"),
@@ -25,21 +27,23 @@ SCRATCH = {
     "wp": ("sbuf", [128, 128 * O], "uint8"),
     "rc": ("sbuf", [128, N * TOK], "float8_e4m3fn_x4"),
     "rs": ("sbuf", [128, N * TOK], "uint8"),
-    "hc": ("sbuf", [128, TOK], "float8_e4m3fn_x4"),
-    "hs": ("sbuf", [128, TOK], "uint8"),
+    "hc": ("sbuf", [128, 2 * TOK], "float8_e4m3fn_x4"),
+    "hs": ("sbuf", [128, 2 * TOK], "uint8"),
     "vt": ("sbuf", [128, 4 * TOK], "bfloat16"),
     "vc": ("sbuf", [128, TOK], "float8_e4m3fn_x4"),
     "vs": ("sbuf", [128, TOK], "uint8"),
     "yo": ("sbuf", [128, O * TOK], "float32"),
     "ps": ("psum", [128, 512 * 6], "float32"),
 }
+for _i in range(4):
+    SCRATCH["tb%d" % _i] = ("sbuf", [128, 4 * K], "bfloat16")
 for _i in range(N):
     SCRATCH["h%d" % _i] = ("sbuf", [128, 4 * TOK], "bfloat16")
 for _i in range(N - 1):
     SCRATCH["qc%d" % _i] = ("sbuf", [128, TOK], "float8_e4m3fn_x4")
     SCRATCH["qs%d" % _i] = ("sbuf", [128, TOK], "uint8")
 
-SEMAPHORES = ["idl", "tbl", "wl", "v", "s", "t", "ga", "lists", "sent", "hcode", "hplane", "yd"] + ["arr%d" % q for q in range(N)]
+SEMAPHORES = ["idl", "tbl", "wl", "v", "s", "t", "ga", "lists0", "lists1", "sent", "hcode0", "hplane0", "hcode1", "hplane1", "yd"] + ["arr%d" % q for q in range(N)]
 
 
 def bits(m):
@@ -53,11 +57,11 @@ def plan(core, T, topo):
     mate = [d for d in ring if topo.mates(ch, topo.chip(T.cores[d]))]
     plane = [d for d in ring if topo.same_plane(ch, topo.chip(T.cores[d]))]
     far = [d for d in ring if d not in mate and d not in plane]
-    help_ = [c for c in topo.cores_of(core) if c != core and all(topo.may_write(c, T.cores[d]) for d in far)]
-    help_.sort(key=lambda c: (topo.die(c) == topo.die(core), c))
-    relayed = [(d, help_[i]) for i, d in enumerate(far)]
-    direct = [(d, None) for d in plane[:2] + mate + plane[2:]]
-    return relayed[:2] + direct[:1] + relayed[2:] + direct[1:]
+    help_ = [c for c in topo.cores_of(core)
+             if topo.die(c) != topo.die(core) and all(topo.may_write(c, T.cores[d]) for d in far)]
+    relayed = [(d, help_[i % len(help_)], i // len(help_)) for i, d in enumerate(far)]
+    direct = [(d, None, 0) for d in plane[:2] + mate + plane[2:]]
+    return relayed[:2] + direct[:2] + relayed[2:] + direct[2:]
 
 
 def rank_program(g, core, T, topo):
@@ -69,10 +73,11 @@ def rank_program(g, core, T, topo):
 
 
 def helper_program(g, core, T, topo):
+    total = 0
     for src in T.cores:
         if topo.chip(src) != topo.chip(core):
             continue
-        for d, h in plan(src, T, topo):
+        for d, h, k in plan(src, T, topo):
             if h != core:
                 continue
             q = T.rank_of(src)
@@ -81,11 +86,13 @@ def helper_program(g, core, T, topo):
             n_in = bits(local_mask(src, core, T, topo))
             m = topo.mask(core, dst)
             arr = T.sem["arr%d" % q]
-            g.wait_ge(T.sem.hcode, n_in)
-            g.remote_dma(T.rc[:, TOK * q:TOK * q + TOK].bitcast(dt.uint8), T.hc[:, 0:TOK].bitcast(dt.uint8), arr, T.sem.sent, pid, rid, m)
-            g.wait_ge(T.sem.hplane, n_in)
-            g.remote_dma(T.rs[:, TOK * q:TOK * q + TOK], T.hs[:, 0:TOK], arr, T.sem.sent, pid, rid, m)
-            g.wait_ge(T.sem.sent, 2 * bits(m))
+            g.wait_ge(T.sem["hcode%d" % k], n_in)
+            g.remote_dma(T.rc[:, TOK * q:TOK * q + TOK].bitcast(dt.uint8), T.hc[:, TOK * k:TOK * k + TOK].bitcast(dt.uint8), arr, T.sem.sent, pid, rid, m)
+            g.wait_ge(T.sem["hplane%d" % k], n_in)
+            g.remote_dma(T.rs[:, TOK * q:TOK * q + TOK], T.hs[:, TOK * k:TOK * k + TOK], arr, T.sem.sent, pid, rid, m)
+            total += 2 * bits(m)
+    if total:
+        g.wait_ge(T.sem.sent, total)
 
 
 def local_mask(src, helper, T, topo):
@@ -94,6 +101,16 @@ def local_mask(src, helper, T, topo):
         if topo.chip(c) != topo.chip(src):
             off |= topo.mask(src, c)
     return topo.mask(src, helper) & ~off
+
+
+def chain(r, T, topo):
+    def turn(q):
+        if q == r:
+            return N
+        p = plan(T.cores[q], T, topo)
+        i = [u[0] for u in p].index(r)
+        return i + (2 if p[i][1] is None else 5)
+    return sorted([0, 1], key=turn) + list(range(2, N))
 
 
 def owner_program(g, core, r, T, topo):
@@ -118,93 +135,127 @@ def owner_program(g, core, r, T, topo):
 
     for i in range(8):
         (syn if i < 4 else sca).dma_start(T.ids8[16 * i:16 * i + 16, :], T.ids[:, :]).then_inc(T.sem.idl, 16)
-    syn.dma_start(T.tbs[:, :], T.tb[:, :]).then_inc(T.sem.tbl, 16)
-    sca.dma_start(T.ws[:, :], T.w[:, :]).then_inc(T.sem.wl, 16)
+    syn.dma_start(T.tb0[:, :], T.tb[:, :]).then_inc(T.sem.tbl, 16)
 
     n_ones = done("v", vec.memset(T.ones[:, :], 1.0))
     g.wait_ge(T.sem.v, n_ones)
     g.affine_select(T.ez[:, :], T.ones[:, :], [[1, 520]], A.is_equal, 0.0, -4, -4).then_inc(T.sem.ga, 1)
 
     g.wait_ge(T.sem.idl, 128)
-    ids_, dsts, mask = [], [], None
-    for d in others:
-        dst = T.cores[d]
-        rid, pid, _ = topo.addr(dst)
-        slot = r if r < d else r - 1
-        ids_.append(DstId(rid=rid, pnc=pid))
-        dsts.append(T.lst[:, 16 * slot:16 * slot + 16])
-        m = topo.mask(core, dst)
-        mask = m if mask is None else mask & m
-    sent = bits(mask)
-    g.remote_dma_fused([RemoteDMATransfer(dst_ids=ids_, dma_engine_mask=mask, remote_sem=T.sem.lists, srcs=[T.ids8[:, :]], dsts=dsts)], local_sem=T.sem.sent)
+    sent = 0
+    place = {d: [u[0] for u in plan(T.cores[d], T, topo)].index(r) for d in others}
+    for k in range(2):
+        ids_, dsts, mask = [], [], None
+        for d in sorted(others, key=lambda x: place[x]):
+            if (place[d] >= EARLY) != bool(k):
+                continue
+            dst = T.cores[d]
+            rid, pid, _ = topo.addr(dst)
+            ids_.append(DstId(rid=rid, pnc=pid))
+            dsts.append(T.lst[:, 16 * place[d]:16 * place[d] + 16])
+            m = topo.mask(core, dst)
+            mask = m if mask is None else mask & m
+        sent += bits(mask)
+        g.remote_dma_fused([RemoteDMATransfer(dst_ids=ids_, dma_engine_mask=mask, remote_sem=T.sem["lists%d" % k], srcs=[T.ids8[:, :]], dsts=dsts)], local_sem=T.sem.sent)
+    each = bits(mask)
+    state = {"sent": sent}
 
     vec.wait_ge(T.sem.ga, 1)
     for b in range(4):
         n_e = done("v", vec.quantize_mx(T.ec[:, 128 * b:128 * b + 128], T.es[:, 128 * b:128 * b + 128], T.ez[:, 4 - b:4 - b + 512]))
 
-    def hashes(src, x, y, off, w):
-        n = done("v", vec.tensor_scalar(x[:, :], src[:, :], HA[r], HB[r], A.mult, A.add))
+    def hashes(src, x, y, off, a, b):
+        n = done("v", vec.tensor_scalar(x[:, a:b], src[:, a:b], HA[r], HB[r], A.mult, A.add))
         need(vec, "v", "v", n)
-        n = done("v", vec.tensor_scalar(y[:, :], x[:, :], 3, 4 * (K - 1), A.arith_shift_right, A.bitwise_and))
+        n = done("v", vec.tensor_scalar(y[:, a:b], x[:, a:b], 3, 4 * (K - 1), A.arith_shift_right, A.bitwise_and))
         need(vec, "v", "v", n)
-        return [done("v", vec.tensor_scalar(off[:, w * t:w * t + w], y[:, :], t, None, A.add)) for t in range(4)]
-
-    def gather(h, off, w, c, ns, outs, n_off):
-        win = T.tbs[:, 0:4 * K]
-        for t in range(4):
-            o = win.indirect(off[:, w * t + c:w * t + c + 16])
-            if t < ns:
-                need(sca, "s", "v", n_off[t])
-                n_s = done("s", sca.activation(h[:, t:4 * TOK:4], o, COPY))
-            else:
-                need(vec, "v", "v", n_off[t])
-                n_v = done("v", vec.tensor_copy(h[:, t:4 * TOK:4], o))
-        need(vec, "v", "v", n_v)
-        need(vec, "v", "s", n_s)
-        return done("v", vec.quantize_mx(outs[0], outs[1], h[:, 0:4 * TOK]))
+        return done("v", vec.tensor_copy(off[:, a:b], y[:, a:b]))
 
     vec.wait_ge(T.sem.idl, 128)
-    n_off = hashes(T.ids8, T.ox, T.oy, T.oo, 16)
-    vec.wait_ge(T.sem.tbl, 16)
+    n_oo = hashes(T.ids8, T.ox, T.oy, T.oo, 0, 16)
     sca.wait_ge(T.sem.tbl, 16)
-    n_own = gather(T["h%d" % (N - 1)], T.oo, 16, 0, 2,
-                   (T.rc[:, TOK * r:TOK * r + TOK], T.rs[:, TOK * r:TOK * r + TOK]), n_off)
+    moved = {1: ("s", done("s", sca.activation(T.tb1[:, 0:WIN], T.tb0[:, 1:1 + WIN], COPY)))}
+    vec.wait_ge(T.sem.tbl, 16)
+    for t in (2, 3):
+        moved[t] = ("v", done("v", vec.tensor_copy(T["tb%d" % t][:, 0:WIN], T.tb0[:, t:t + WIN])))
 
-    vec.wait_ge(T.sem.lists, sent * (N - 1))
-    n_off = hashes(T.lst, T.lx, T.ly, T.lo, LW)
-    for i, (d, helper) in enumerate(order):
-        qc, qs = T["qc%d" % i], T["qs%d" % i]
-        slot = d if d < r else d - 1
-        n_q = gather(T["h%d" % i], T.lo, LW, 16 * slot, 3 if i == len(order) - 1 else 2, (qc[:, 0:TOK], qs[:, 0:TOK]), n_off)
-        g.wait_ge(T.sem.v, n_q)
-        if helper is None:
-            dst = T.cores[d]
+    def pick(eng, me, h, off, t, n_off):
+        need(eng, me, "v", n_off)
+        if t:
+            need(eng, me, moved[t][0], moved[t][1])
+        o, i = h[:, t:4 * TOK:4], T["tb%d" % t][:, 0:WIN].indirect(off)
+        return done(me, sca.activation(o, i, COPY) if me == "s" else vec.tensor_copy(o, i))
+
+    def pack(u):
+        need(vec, "v", "v", u["v"])
+        need(vec, "v", "s", u["s"])
+        return done("v", vec.quantize_mx(u["c"], u["p"], u["h"][:, 0:4 * TOK]))
+
+    def pack_and_send(u):
+        g.wait_ge(T.sem.v, pack(u))
+        k = u["k"]
+        if u["via"] is None:
+            dst = T.cores[u["to"]]
             oc, op = T.rc[:, TOK * r:TOK * r + TOK], T.rs[:, TOK * r:TOK * r + TOK]
             sc = sp = T.sem["arr%d" % r]
             m = topo.mask(core, dst)
         else:
-            dst = helper
-            oc, op = T.hc[:, 0:TOK], T.hs[:, 0:TOK]
-            sc, sp = T.sem.hcode, T.sem.hplane
-            m = local_mask(core, helper, T, topo)
+            dst = u["via"]
+            oc, op = T.hc[:, TOK * k:TOK * k + TOK], T.hs[:, TOK * k:TOK * k + TOK]
+            sc, sp = T.sem["hcode%d" % k], T.sem["hplane%d" % k]
+            m = local_mask(core, dst, T, topo)
         rid, pid, _ = topo.addr(dst)
-        g.remote_dma(oc.bitcast(dt.uint8), qc[:, 0:TOK].bitcast(dt.uint8), sc, T.sem.sent, pid, rid, m)
-        g.remote_dma(op, qs[:, 0:TOK], sp, T.sem.sent, pid, rid, m)
-        sent += 2 * bits(m)
+        g.remote_dma(oc.bitcast(dt.uint8), u["c"].bitcast(dt.uint8), sc, T.sem.sent, pid, rid, m)
+        g.remote_dma(op, u["p"], sp, T.sem.sent, pid, rid, m)
+        state["sent"] += 2 * bits(m)
 
+    n_of = {}
+
+    def listed(k, a, b):
+        vec.wait_ge(T.sem["lists%d" % k], each * (b - a))
+        n = hashes(T.lst, T.lx, T.ly, T.lo, 16 * a, 16 * b)
+        for i in range(a, b):
+            n_of[i] = n
+
+    listed(0, 0, EARLY)
+    before = None
+    for i, (d, helper, k) in enumerate(order):
+        u = {"h": T["h%d" % i], "c": T["qc%d" % i][:, 0:TOK], "p": T["qs%d" % i][:, 0:TOK], "to": d, "via": helper, "k": k}
+        off = T.lo[:, 16 * i:16 * i + 16]
+        for t in range(SHARE[i]):
+            u["s"] = pick(sca, "s", u["h"], off, t, n_of[i])
+        for t in range(SHARE[i], 4):
+            u["v"] = pick(vec, "v", u["h"], off, t, n_of[i])
+            if before is not None:
+                pack_and_send(before)
+                before = None
+        before = u
+        if i == EARLY - 1:
+            listed(1, EARLY, N - 1)
+    pack_and_send(before)
+
+    u = {"h": T["h%d" % (N - 1)], "c": T.rc[:, TOK * r:TOK * r + TOK], "p": T.rs[:, TOK * r:TOK * r + TOK]}
+    for t in range(4):
+        if t < 2:
+            u["s"] = pick(sca, "s", u["h"], T.oo[:, 0:16], t, n_oo)
+        else:
+            u["v"] = pick(vec, "v", u["h"], T.oo[:, 0:16], t, n_oo)
+    n_own = pack(u)
+    syn.wait_ge(T.sem.lists0, each * EARLY)
+    syn.dma_start(T.ws[:, :], T.w[:, :]).then_inc(T.sem.wl, 16)
     vec.wait_ge(T.sem.wl, 16)
     n_w = done("v", vec.quantize_mx(T.wc[:, 0:128 * O], T.wp[:, 0:128 * O], T.ws[:, 0:512 * O]))
 
     need(ten, "t", "v", n_e)
     n_t = [0] * 4
-    for q in range(N):
+    for k, q in enumerate(chain(r, T, topo)):
         if q == r:
             need(ten, "t", "v", n_own)
         else:
-            ten.wait_ge(T.sem["arr%d" % q], 2 * bits(mask))
+            ten.wait_ge(T.sem["arr%d" % q], 2 * each)
         for b in range(4):
             n_t[b] = done("t", ten.matmul_mx(T.ps[:, 512 * b:512 * b + TOK], T.ec[:, 128 * b:128 * b + 128], T.es[:, 128 * b:128 * b + 128],
-                                             T.rc[:, TOK * q:TOK * q + TOK], T.rs[:, TOK * q:TOK * q + TOK], q == 0, q == N - 1))
+                                             T.rc[:, TOK * q:TOK * q + TOK], T.rs[:, TOK * q:TOK * q + TOK], k == 0, k == N - 1))
 
     for b in range(4):
         o, i = T.vt[:, b:4 * TOK:4], T.ps[:, 512 * b:512 * b + TOK]
@@ -230,4 +281,4 @@ def owner_program(g, core, r, T, topo):
     need(syn, "y", "v", n_v)
     syn.dma_start(T.y[:, TOK:2 * TOK], T.yo[:, TOK:2 * TOK]).then_inc(T.sem.yd, 16)
     syn.wait_ge(T.sem.yd, 32)
-    g.wait_ge(T.sem.sent, sent)
+    g.wait_ge(T.sem.sent, state["sent"])

@@ -2,11 +2,12 @@ from concourse.bass import DstId, RemoteDMATransfer
 from concourse.mybir import dt, AluOpType, ActivationFunctionType
 
 N, TOK, K, O = 8, 256, 256, 2
+H = TOK // 2
 HA = (1237, 1811, 947, 1543, 2017, 733, 1409, 1699)
 HB = (40503, 12289, 58111, 3571, 27644, 61007, 19211, 50021)
-EARLY = 3
-SHARE = (2, 2, 3, 2, 2, 3, 2)
-LW = 16 * (N - 1)
+SHARE = (2, 3, 2, 3, 2, 3, 2)
+SLOTS = 2 * (N - 1)
+LH = H // 16
 WIN = 4 * K - 3
 
 SCRATCH = {
@@ -14,10 +15,10 @@ SCRATCH = {
     "ox": ("sbuf", [128, 16], "int32"),
     "oy": ("sbuf", [128, 16], "int32"),
     "oo": ("sbuf", [128, 16], "uint16"),
-    "lst": ("sbuf", [128, LW], "int32"),
-    "lx": ("sbuf", [128, LW], "int32"),
-    "ly": ("sbuf", [128, LW], "int32"),
-    "lo": ("sbuf", [128, LW], "uint16"),
+    "lst": ("sbuf", [128, LH * SLOTS], "int32"),
+    "lx": ("sbuf", [128, LH * SLOTS], "int32"),
+    "ly": ("sbuf", [128, LH * SLOTS], "int32"),
+    "lo": ("sbuf", [128, LH * SLOTS], "uint16"),
     "ws": ("sbuf", [128, 512 * O], "bfloat16"),
     "ones": ("sbuf", [128, 520], "bfloat16"),
     "ez": ("sbuf", [128, 520], "bfloat16"),
@@ -27,13 +28,14 @@ SCRATCH = {
     "wp": ("sbuf", [128, 128 * O], "uint8"),
     "rc": ("sbuf", [128, N * TOK], "float8_e4m3fn_x4"),
     "rs": ("sbuf", [128, N * TOK], "uint8"),
-    "hc": ("sbuf", [128, 2 * TOK], "float8_e4m3fn_x4"),
-    "hs": ("sbuf", [128, 2 * TOK], "uint8"),
-    "vt": ("sbuf", [128, 4 * TOK], "bfloat16"),
+    "hc": ("sbuf", [128, 4 * TOK], "float8_e4m3fn_x4"),
+    "hs": ("sbuf", [128, 4 * TOK], "uint8"),
+    "vt0": ("sbuf", [128, 4 * H], "bfloat16"),
+    "vt1": ("sbuf", [128, 4 * H], "bfloat16"),
     "vc": ("sbuf", [128, TOK], "float8_e4m3fn_x4"),
     "vs": ("sbuf", [128, TOK], "uint8"),
     "yo": ("sbuf", [128, O * TOK], "float32"),
-    "ps": ("psum", [128, 512 * 6], "float32"),
+    "ps": ("psum", [128, 512 * 8], "float32"),
 }
 for _i in range(4):
     SCRATCH["tb%d" % _i] = ("sbuf", [128, 4 * K], "bfloat16")
@@ -43,11 +45,17 @@ for _i in range(N - 1):
     SCRATCH["qc%d" % _i] = ("sbuf", [128, TOK], "float8_e4m3fn_x4")
     SCRATCH["qs%d" % _i] = ("sbuf", [128, TOK], "uint8")
 
-SEMAPHORES = ["idl", "tbl", "wl", "v", "s", "t", "ga", "lists0", "lists1", "sent", "hcode0", "hplane0", "hcode1", "hplane1", "yd"] + ["arr%d" % q for q in range(N)]
+SEMAPHORES = ["idl", "tbl", "wl", "v", "s", "t", "ga", "lists0", "lists1", "lists2", "sent", "yd"]
+SEMAPHORES += ["hcode%d" % i for i in range(8)] + ["hplane%d" % i for i in range(8)]
+SEMAPHORES += ["arr%d_%d" % (h, q) for h in range(2) for q in range(N)]
 
 
 def bits(m):
     return bin(m).count("1")
+
+
+def as_mask(engines):
+    return sum(1 << e for e in engines)
 
 
 def plan(core, T, topo):
@@ -59,9 +67,38 @@ def plan(core, T, topo):
     far = [d for d in ring if d not in mate and d not in plane]
     help_ = [c for c in topo.cores_of(core)
              if topo.die(c) != topo.die(core) and all(topo.may_write(c, T.cores[d]) for d in far)]
-    relayed = [(d, help_[i % len(help_)], i // len(help_)) for i, d in enumerate(far)]
-    direct = [(d, None, 0) for d in plane[:2] + mate + plane[2:]]
-    return relayed[:2] + direct[:2] + relayed[2:] + direct[2:]
+    off = {e for d in ring for e in topo.engines(core, T.cores[d])}
+    helper = {d: help_[i % len(help_)] for i, d in enumerate(far)}
+    D = plane + mate
+    first = far[:2] + D + far[2:]
+    second = far[2:] + far[:2] + D
+    slot = {(d, 0): i for i, d in enumerate(first)}
+    slot.update({(d, 1): N - 1 + i for i, d in enumerate(second)})
+    shape = [[(far[0], 0), (far[1], 0)], [(D[0], 0), (D[1], 0)], [(far[2], None)], [(D[2], 0), (D[3], 0)],
+             [(far[0], 1), (far[1], 1)], [(D[0], 1), (D[1], 1)], [(D[2], 1), (D[3], 1)]]
+    used = {c: [0, 0] for c in help_}
+    units = []
+    for u in shape:
+        pieces = []
+        for i, (d, half) in enumerate(u):
+            n = TOK if half is None else H
+            via = helper.get(d)
+            if via is None:
+                e = topo.engines(core, T.cores[d])
+            else:
+                e = [x for x in topo.engines(core, via) if x not in off]
+            w = len(e) // len(u)
+            p = {"to": d, "half": half, "slot": slot[(d, half or 0)], "col": i * H, "n": n, "via": via, "mask": as_mask(e[i * w:i * w + w])}
+            if via is not None:
+                p["place"], p["at"] = used[via]
+                used[via] = [p["place"] + 1, p["at"] + n]
+            pieces.append(p)
+        units.append(pieces)
+    return units, slot
+
+
+def column(q, half):
+    return TOK * q + H * (half or 0)
 
 
 def rank_program(g, core, T, topo):
@@ -77,40 +114,36 @@ def helper_program(g, core, T, topo):
     for src in T.cores:
         if topo.chip(src) != topo.chip(core):
             continue
-        for d, h, k in plan(src, T, topo):
-            if h != core:
-                continue
-            q = T.rank_of(src)
-            dst = T.cores[d]
+        q = T.rank_of(src)
+        for p in [p for u in plan(src, T, topo)[0] for p in u if p["via"] == core]:
+            dst = T.cores[p["to"]]
             rid, pid, _ = topo.addr(dst)
-            n_in = bits(local_mask(src, core, T, topo))
+            n_in = bits(p["mask"])
             m = topo.mask(core, dst)
-            arr = T.sem["arr%d" % q]
-            g.wait_ge(T.sem["hcode%d" % k], n_in)
-            g.remote_dma(T.rc[:, TOK * q:TOK * q + TOK].bitcast(dt.uint8), T.hc[:, TOK * k:TOK * k + TOK].bitcast(dt.uint8), arr, T.sem.sent, pid, rid, m)
-            g.wait_ge(T.sem["hplane%d" % k], n_in)
-            g.remote_dma(T.rs[:, TOK * q:TOK * q + TOK], T.hs[:, TOK * k:TOK * k + TOK], arr, T.sem.sent, pid, rid, m)
+            arr = T.sem["arr%d_%d" % (p["half"] or 0, q)]
+            a, b, n = column(q, p["half"]), p["at"], p["n"]
+            g.wait_ge(T.sem["hcode%d" % p["place"]], n_in)
+            g.remote_dma(T.rc[:, a:a + n].bitcast(dt.uint8), T.hc[:, b:b + n].bitcast(dt.uint8), arr, T.sem.sent, pid, rid, m)
+            g.wait_ge(T.sem["hplane%d" % p["place"]], n_in)
+            g.remote_dma(T.rs[:, a:a + n], T.hs[:, b:b + n], arr, T.sem.sent, pid, rid, m)
             total += 2 * bits(m)
     if total:
         g.wait_ge(T.sem.sent, total)
 
 
-def local_mask(src, helper, T, topo):
-    off = 0
-    for c in T.cores:
-        if topo.chip(c) != topo.chip(src):
-            off |= topo.mask(src, c)
-    return topo.mask(src, helper) & ~off
+def arrival(q, r, half, T, topo):
+    for i, u in enumerate(plan(T.cores[q], T, topo)[0]):
+        for p in u:
+            if p["to"] == r and p["half"] in (half, None):
+                if p["via"] is None:
+                    m, hops = p["mask"], 2
+                else:
+                    m, hops = topo.mask(p["via"], T.cores[r]), 4
+                return i + hops, "arr%d_%d" % (p["half"] or 0, q), 2 * bits(m)
 
 
-def chain(r, T, topo):
-    def turn(q):
-        if q == r:
-            return N
-        p = plan(T.cores[q], T, topo)
-        i = [u[0] for u in p].index(r)
-        return i + (2 if p[i][1] is None else 5)
-    return sorted([0, 1], key=turn) + list(range(2, N))
+def chain(r, half, T, topo):
+    return sorted([0, 1], key=lambda q: 0 if q == r else arrival(q, r, half, T, topo)[0]) + list(range(2, N))
 
 
 def owner_program(g, core, r, T, topo):
@@ -130,7 +163,7 @@ def owner_program(g, core, r, T, topo):
             queue.wait_ge(T.sem[name], val)
             seen[(me, name)] = val
 
-    order = plan(core, T, topo)
+    units, _ = plan(core, T, topo)
     others = [d for d in range(N) if d != r]
 
     for i in range(8):
@@ -141,22 +174,24 @@ def owner_program(g, core, r, T, topo):
     g.wait_ge(T.sem.v, n_ones)
     g.affine_select(T.ez[:, :], T.ones[:, :], [[1, 520]], A.is_equal, 0.0, -4, -4).then_inc(T.sem.ga, 1)
 
+    GROUPS = ((0, 4), (4, N - 1), (N - 1, SLOTS))
     g.wait_ge(T.sem.idl, 128)
     sent = 0
-    place = {d: [u[0] for u in plan(T.cores[d], T, topo)].index(r) for d in others}
-    for k in range(2):
-        ids_, dsts, mask = [], [], None
-        for d in sorted(others, key=lambda x: place[x]):
-            if (place[d] >= EARLY) != bool(k):
+    mine = {d: plan(T.cores[d], T, topo)[1] for d in others}
+    for k, (lo_, hi_) in enumerate(GROUPS):
+        ids_, dsts, mask, half = [], [], None, k // 2
+        for d in sorted(others, key=lambda x: mine[x][(r, half)]):
+            s = mine[d][(r, half)]
+            if not lo_ <= s < hi_:
                 continue
             dst = T.cores[d]
             rid, pid, _ = topo.addr(dst)
             ids_.append(DstId(rid=rid, pnc=pid))
-            dsts.append(T.lst[:, 16 * place[d]:16 * place[d] + 16])
+            dsts.append(T.lst[:, LH * s:LH * s + LH])
             m = topo.mask(core, dst)
             mask = m if mask is None else mask & m
         sent += bits(mask)
-        g.remote_dma_fused([RemoteDMATransfer(dst_ids=ids_, dma_engine_mask=mask, remote_sem=T.sem["lists%d" % k], srcs=[T.ids8[:, :]], dsts=dsts)], local_sem=T.sem.sent)
+        g.remote_dma_fused([RemoteDMATransfer(dst_ids=ids_, dma_engine_mask=mask, remote_sem=T.sem["lists%d" % k], srcs=[T.ids8[:, LH * half:LH * half + LH]], dsts=dsts)], local_sem=T.sem.sent)
     each = bits(mask)
     state = {"sent": sent}
 
@@ -171,14 +206,6 @@ def owner_program(g, core, r, T, topo):
         need(vec, "v", "v", n)
         return done("v", vec.tensor_copy(off[:, a:b], y[:, a:b]))
 
-    vec.wait_ge(T.sem.idl, 128)
-    n_oo = hashes(T.ids8, T.ox, T.oy, T.oo, 0, 16)
-    sca.wait_ge(T.sem.tbl, 16)
-    moved = {1: ("s", done("s", sca.activation(T.tb1[:, 0:WIN], T.tb0[:, 1:1 + WIN], COPY)))}
-    vec.wait_ge(T.sem.tbl, 16)
-    for t in (2, 3):
-        moved[t] = ("v", done("v", vec.tensor_copy(T["tb%d" % t][:, 0:WIN], T.tb0[:, t:t + WIN])))
-
     def pick(eng, me, h, off, t, n_off):
         need(eng, me, "v", n_off)
         if t:
@@ -186,99 +213,149 @@ def owner_program(g, core, r, T, topo):
         o, i = h[:, t:4 * TOK:4], T["tb%d" % t][:, 0:WIN].indirect(off)
         return done(me, sca.activation(o, i, COPY) if me == "s" else vec.tensor_copy(o, i))
 
+    vec.wait_ge(T.sem.idl, 128)
+    n_oo = hashes(T.ids8, T.ox, T.oy, T.oo, 0, 16)
+    own = {"h": T["h%d" % (N - 1)], "c": T.rc[:, TOK * r:TOK * r + TOK], "p": T.rs[:, TOK * r:TOK * r + TOK]}
+    moved = {}
+    sca.wait_ge(T.sem.tbl, 16)
+    moved[1] = ("s", done("s", sca.activation(T.tb1[:, 0:WIN], T.tb0[:, 1:1 + WIN], COPY)))
+    vec.wait_ge(T.sem.tbl, 16)
+    for t in (2, 3):
+        moved[t] = ("v", done("v", vec.tensor_copy(T["tb%d" % t][:, 0:WIN], T.tb0[:, t:t + WIN])))
+    for t in (0, 1):
+        own["s"] = pick(sca, "s", own["h"], T.oo[:, 0:16], t, n_oo)
+    for t in (2, 3):
+        own["v"] = pick(vec, "v", own["h"], T.oo[:, 0:16], t, n_oo)
+
     def pack(u):
         need(vec, "v", "v", u["v"])
         need(vec, "v", "s", u["s"])
         return done("v", vec.quantize_mx(u["c"], u["p"], u["h"][:, 0:4 * TOK]))
 
     def pack_and_send(u):
-        g.wait_ge(T.sem.v, pack(u))
-        k = u["k"]
-        if u["via"] is None:
-            dst = T.cores[u["to"]]
-            oc, op = T.rc[:, TOK * r:TOK * r + TOK], T.rs[:, TOK * r:TOK * r + TOK]
-            sc = sp = T.sem["arr%d" % r]
-            m = topo.mask(core, dst)
-        else:
-            dst = u["via"]
-            oc, op = T.hc[:, TOK * k:TOK * k + TOK], T.hs[:, TOK * k:TOK * k + TOK]
-            sc, sp = T.sem["hcode%d" % k], T.sem["hplane%d" % k]
-            m = local_mask(core, dst, T, topo)
-        rid, pid, _ = topo.addr(dst)
-        g.remote_dma(oc.bitcast(dt.uint8), u["c"].bitcast(dt.uint8), sc, T.sem.sent, pid, rid, m)
-        g.remote_dma(op, u["p"], sp, T.sem.sent, pid, rid, m)
-        state["sent"] += 2 * bits(m)
+        n = pack(u)
+        if "pieces" not in u:
+            u["n"] = n
+            return
+        g.wait_ge(T.sem.v, n)
+        codes, planes = [], []
+        for p in u["pieces"]:
+            a, c, w = column(r, p["half"]), p["col"], p["n"]
+            if p["via"] is None:
+                dst, oc, op = T.cores[p["to"]], T.rc[:, a:a + w], T.rs[:, a:a + w]
+                sc = sp = T.sem["arr%d_%d" % (p["half"] or 0, r)]
+            else:
+                b = p["at"]
+                dst, oc, op = p["via"], T.hc[:, b:b + w], T.hs[:, b:b + w]
+                sc, sp = T.sem["hcode%d" % p["place"]], T.sem["hplane%d" % p["place"]]
+            rid, pid, _ = topo.addr(dst)
+            to = [DstId(rid=rid, pnc=pid)]
+            codes.append(RemoteDMATransfer(dst_ids=to, dma_engine_mask=p["mask"], remote_sem=sc, srcs=[u["c"][c:c + w].bitcast(dt.uint8)] if False else [u["qc"][:, c:c + w].bitcast(dt.uint8)], dsts=[oc.bitcast(dt.uint8)]))
+            planes.append(RemoteDMATransfer(dst_ids=to, dma_engine_mask=p["mask"], remote_sem=sp, srcs=[u["qs"][:, c:c + w]], dsts=[op]))
+            state["sent"] += 2 * bits(p["mask"])
+        g.remote_dma_fused(codes, local_sem=T.sem.sent)
+        g.remote_dma_fused(planes, local_sem=T.sem.sent)
 
     n_of = {}
 
-    def listed(k, a, b):
-        vec.wait_ge(T.sem["lists%d" % k], each * (b - a))
-        n = hashes(T.lst, T.lx, T.ly, T.lo, 16 * a, 16 * b)
+    def listed(ks):
+        for k in ks:
+            vec.wait_ge(T.sem["lists%d" % k], each * (GROUPS[k][1] - GROUPS[k][0]))
+        a, b = GROUPS[ks[0]][0], GROUPS[ks[-1]][1]
+        n = hashes(T.lst, T.lx, T.ly, T.lo, LH * a, LH * b)
         for i in range(a, b):
             n_of[i] = n
 
-    listed(0, 0, EARLY)
-    before = None
-    for i, (d, helper, k) in enumerate(order):
-        u = {"h": T["h%d" % i], "c": T["qc%d" % i][:, 0:TOK], "p": T["qs%d" % i][:, 0:TOK], "to": d, "via": helper, "k": k}
-        off = T.lo[:, 16 * i:16 * i + 16]
+    listed([0])
+    before = own
+    for i, pieces in enumerate(units):
+        u = {"h": T["h%d" % i], "qc": T["qc%d" % i], "qs": T["qs%d" % i], "c": T["qc%d" % i][:, 0:TOK], "p": T["qs%d" % i][:, 0:TOK], "pieces": pieces}
+        s = pieces[0]["slot"]
+        off = T.lo[:, LH * s:LH * s + 2 * LH]
         for t in range(SHARE[i]):
-            u["s"] = pick(sca, "s", u["h"], off, t, n_of[i])
+            u["s"] = pick(sca, "s", u["h"], off, t, n_of[s + 1])
         for t in range(SHARE[i], 4):
-            u["v"] = pick(vec, "v", u["h"], off, t, n_of[i])
+            u["v"] = pick(vec, "v", u["h"], off, t, n_of[s + 1])
             if before is not None:
                 pack_and_send(before)
                 before = None
         before = u
-        if i == EARLY - 1:
-            listed(1, EARLY, N - 1)
+        if i == 1:
+            listed([1, 2])
     pack_and_send(before)
 
-    u = {"h": T["h%d" % (N - 1)], "c": T.rc[:, TOK * r:TOK * r + TOK], "p": T.rs[:, TOK * r:TOK * r + TOK]}
-    for t in range(4):
-        if t < 2:
-            u["s"] = pick(sca, "s", u["h"], T.oo[:, 0:16], t, n_oo)
-        else:
-            u["v"] = pick(vec, "v", u["h"], T.oo[:, 0:16], t, n_oo)
-    n_own = pack(u)
-    syn.wait_ge(T.sem.lists0, each * EARLY)
+    syn.wait_ge(T.sem.lists0, each * GROUPS[0][1])
     syn.dma_start(T.ws[:, :], T.w[:, :]).then_inc(T.sem.wl, 16)
     vec.wait_ge(T.sem.wl, 16)
     n_w = done("v", vec.quantize_mx(T.wc[:, 0:128 * O], T.wp[:, 0:128 * O], T.ws[:, 0:512 * O]))
 
     need(ten, "t", "v", n_e)
-    n_t = [0] * 4
-    for k, q in enumerate(chain(r, T, topo)):
-        if q == r:
-            need(ten, "t", "v", n_own)
-        else:
-            ten.wait_ge(T.sem["arr%d" % q], 2 * each)
-        for b in range(4):
-            n_t[b] = done("t", ten.matmul_mx(T.ps[:, 512 * b:512 * b + TOK], T.ec[:, 128 * b:128 * b + 128], T.es[:, 128 * b:128 * b + 128],
-                                             T.rc[:, TOK * q:TOK * q + TOK], T.rs[:, TOK * q:TOK * q + TOK], k == 0, k == N - 1))
+    waited = {}
 
-    for b in range(4):
-        o, i = T.vt[:, b:4 * TOK:4], T.ps[:, 512 * b:512 * b + TOK]
-        if b % 2 == 0:
-            need(sca, "s", "t", n_t[b])
-            n_s = done("s", sca.activation(o, i, COPY))
+    def add(half, k, q):
+        if q == r:
+            need(ten, "t", "v", own["n"])
         else:
-            need(vec, "v", "t", n_t[b])
-            n_v = done("v", vec.tensor_copy(o, i))
-    need(vec, "v", "v", n_v)
-    need(vec, "v", "s", n_s)
-    n_q = done("v", vec.quantize_mx(T.vc[:, 0:TOK], T.vs[:, 0:TOK], T.vt[:, 0:4 * TOK]))
-    need(ten, "t", "v", n_w)
-    need(ten, "t", "v", n_q)
-    n_y = [done("t", ten.matmul_mx(T.ps[:, 512 * (4 + o):512 * (4 + o) + TOK], T.wc[:, 128 * o:128 * o + 128], T.wp[:, 128 * o:128 * o + 128],
-                                   T.vc[:, 0:TOK], T.vs[:, 0:TOK], True, True)) for o in range(O)]
-    need(sca, "s", "t", n_y[0])
-    n_s = done("s", sca.activation(T.yo[:, 0:TOK], T.ps[:, 2048:2048 + TOK], COPY))
-    need(sca, "s", "s", n_s)
-    sca.dma_start(T.y[:, 0:TOK], T.yo[:, 0:TOK]).then_inc(T.sem.yd, 16)
-    need(vec, "v", "t", n_y[1])
-    n_v = done("v", vec.tensor_copy(T.yo[:, TOK:2 * TOK], T.ps[:, 2560:2560 + TOK]))
-    need(syn, "y", "v", n_v)
-    syn.dma_start(T.y[:, TOK:2 * TOK], T.yo[:, TOK:2 * TOK]).then_inc(T.sem.yd, 16)
-    syn.wait_ge(T.sem.yd, 32)
+            _, sem, n = arrival(q, r, half, T, topo)
+            if sem not in waited:
+                ten.wait_ge(T.sem[sem], n)
+                waited[sem] = n
+        a, n_t = column(q, half), []
+        for b in range(4):
+            c = 512 * (4 * half + b)
+            n_t.append(done("t", ten.matmul_mx(T.ps[:, c:c + H], T.ec[:, 128 * b:128 * b + 128], T.es[:, 128 * b:128 * b + 128],
+                                               T.rc[:, a:a + H], T.rs[:, a:a + H], k == 0, k == N - 1)))
+        return n_t
+
+    def make_v(half, n_t):
+        vt = T["vt%d" % half]
+        for b in range(4):
+            c = 512 * (4 * half + b)
+            o, i = vt[:, b:4 * H:4], T.ps[:, c:c + H]
+            if b % 2 == 0:
+                need(sca, "s", "t", n_t[b])
+                n_s = done("s", sca.activation(o, i, COPY))
+            else:
+                need(vec, "v", "t", n_t[b])
+                n_v = done("v", vec.tensor_copy(o, i))
+        need(vec, "v", "v", n_v)
+        need(vec, "v", "s", n_s)
+        return done("v", vec.quantize_mx(T.vc[:, H * half:H * half + H], T.vs[:, H * half:H * half + H], vt[:, 0:4 * H]))
+
+    def times_w(half, n_q):
+        need(ten, "t", "v", n_w)
+        need(ten, "t", "v", n_q)
+        n = []
+        for o in range(O):
+            c = 512 * (2 * half + o)
+            n.append(done("t", ten.matmul_mx(T.ps[:, c:c + H], T.wc[:, 128 * o:128 * o + 128], T.wp[:, 128 * o:128 * o + 128],
+                                             T.vc[:, H * half:H * half + H], T.vs[:, H * half:H * half + H], True, True)))
+        return n
+
+    def store(half, n_y):
+        y0, y1 = H * half, TOK + H * half
+        c = 1024 * half
+        need(sca, "s", "t", n_y[0])
+        n_s = done("s", sca.activation(T.yo[:, y0:y0 + H], T.ps[:, c:c + H], COPY))
+        need(vec, "v", "t", n_y[1])
+        n_v = done("v", vec.tensor_copy(T.yo[:, y1:y1 + H], T.ps[:, c + 512:c + 512 + H]))
+        if half:
+            need(sca, "s", "s", n_s)
+            sca.dma_start(T.y[:, y0:y0 + H], T.yo[:, y0:y0 + H]).then_inc(T.sem.yd, 16)
+        else:
+            need(syn, "y", "s", n_s)
+            syn.dma_start(T.y[:, y0:y0 + H], T.yo[:, y0:y0 + H]).then_inc(T.sem.yd, 16)
+        need(syn, "y", "v", n_v)
+        syn.dma_start(T.y[:, y1:y1 + H], T.yo[:, y1:y1 + H]).then_inc(T.sem.yd, 16)
+
+    for k, q in enumerate(chain(r, 0, T, topo)):
+        n_a = add(0, k, q)
+    n_q = make_v(0, n_a)
+    for k, q in enumerate(chain(r, 1, T, topo)):
+        n_b = add(1, k, q)
+        if k == 2:
+            n_y = times_w(0, n_q)
+    store(0, n_y)
+    store(1, times_w(1, make_v(1, n_b)))
+    syn.wait_ge(T.sem.yd, 64)
     g.wait_ge(T.sem.sent, state["sent"])

from concourse.bass import DstId, RemoteDMATransfer
from concourse.mybir import dt, AluOpType, ActivationFunctionType

N, TOK, K, O = 8, 256, 256, 2
H = TOK // 2
HA = (1237, 1811, 947, 1543, 2017, 733, 1409, 1699)
HB = (40503, 12289, 58111, 3571, 27644, 61007, 19211, 50021)
SHARE = (2, 3, 2, 3, 2, 3, 2)
SLOTS = 2 * (N - 1)
LH = H // 16
WIN = 4 * K - 3

SCRATCH = {
    "ids8": ("sbuf", [128, 16], "int32"),
    "ox": ("sbuf", [128, 16], "int32"),
    "oy": ("sbuf", [128, 16], "int32"),
    "oo": ("sbuf", [128, 16], "uint16"),
    "lst": ("sbuf", [128, LH * SLOTS], "int32"),
    "lx": ("sbuf", [128, LH * SLOTS], "int32"),
    "ly": ("sbuf", [128, LH * SLOTS], "int32"),
    "lo": ("sbuf", [128, LH * SLOTS], "uint16"),
    "ws": ("sbuf", [128, 512 * O], "bfloat16"),
    "ones": ("sbuf", [128, 520], "bfloat16"),
    "ez": ("sbuf", [128, 520], "bfloat16"),
    "ec": ("sbuf", [128, 512], "float8_e4m3fn_x4"),
    "es": ("sbuf", [128, 512], "uint8"),
    "wc": ("sbuf", [128, 128 * O], "float8_e4m3fn_x4"),
    "wp": ("sbuf", [128, 128 * O], "uint8"),
    "rc": ("sbuf", [128, N * TOK], "float8_e4m3fn_x4"),
    "rs": ("sbuf", [128, N * TOK], "uint8"),
    "hc": ("sbuf", [128, 4 * TOK], "float8_e4m3fn_x4"),
    "hs": ("sbuf", [128, 4 * TOK], "uint8"),
    "vt0": ("sbuf", [128, 4 * H], "bfloat16"),
    "vt1": ("sbuf", [128, 4 * H], "bfloat16"),
    "vc": ("sbuf", [128, TOK], "float8_e4m3fn_x4"),
    "vs": ("sbuf", [128, TOK], "uint8"),
    "yo": ("sbuf", [128, O * TOK], "float32"),
    "ps": ("psum", [128, 512 * 8], "float32"),
}
for _i in range(4):
    SCRATCH["tb%d" % _i] = ("sbuf", [128, 4 * K], "bfloat16")
for _i in range(N):
    SCRATCH["h%d" % _i] = ("sbuf", [128, 4 * TOK], "bfloat16")
for _i in range(N - 1):
    SCRATCH["qc%d" % _i] = ("sbuf", [128, TOK], "float8_e4m3fn_x4")
    SCRATCH["qs%d" % _i] = ("sbuf", [128, TOK], "uint8")

SEMAPHORES = ["idl", "tbl", "wl", "v", "s", "t", "ga", "lists0", "lists1", "lists2", "sent", "yd"]
SEMAPHORES += ["hcode%d" % i for i in range(8)] + ["hplane%d" % i for i in range(8)]
SEMAPHORES += ["arr%d_%d" % (h, q) for h in range(2) for q in range(N)]


def bits(m):
    return bin(m).count("1")


def as_mask(engines):
    return sum(1 << e for e in engines)


def plan(core, T, topo):
    ch = topo.chip(core)
    r = T.rank_of(core)
    ring = [(r + k) % N for k in range(1, N)]
    mate = [d for d in ring if topo.mates(ch, topo.chip(T.cores[d]))]
    plane = [d for d in ring if topo.same_plane(ch, topo.chip(T.cores[d]))]
    far = [d for d in ring if d not in mate and d not in plane]
    help_ = [c for c in topo.cores_of(core)
             if topo.die(c) != topo.die(core) and all(topo.may_write(c, T.cores[d]) for d in far)]
    off = {e for d in ring for e in topo.engines(core, T.cores[d])}
    helper = {d: help_[i % len(help_)] for i, d in enumerate(far)}
    D = plane + mate
    first = far[:2] + D + far[2:]
    second = far[2:] + far[:2] + D
    slot = {(d, 0): i for i, d in enumerate(first)}
    slot.update({(d, 1): N - 1 + i for i, d in enumerate(second)})
    shape = [[(far[0], 0), (far[1], 0)], [(D[0], 0), (D[1], 0)], [(far[2], None)], [(D[2], 0), (D[3], 0)],
             [(far[0], 1), (far[1], 1)], [(D[0], 1), (D[1], 1)], [(D[2], 1), (D[3], 1)]]
    used = {c: [0, 0] for c in help_}
    units = []
    for u in shape:
        pieces = []
        for i, (d, half) in enumerate(u):
            n = TOK if half is None else H
            via = helper.get(d)
            if via is None:
                e = topo.engines(core, T.cores[d])
            else:
                e = [x for x in topo.engines(core, via) if x not in off]
            w = len(e) // len(u)
            p = {"to": d, "half": half, "slot": slot[(d, half or 0)], "col": i * H, "n": n, "via": via, "mask": as_mask(e[i * w:i * w + w])}
            if via is not None:
                p["place"], p["at"] = used[via]
                used[via] = [p["place"] + 1, p["at"] + n]
            pieces.append(p)
        units.append(pieces)
    return units, slot


def column(q, half):
    return TOK * q + H * (half or 0)


def rank_program(g, core, T, topo):
    rank = T.rank_of(core)
    if rank is None:
        helper_program(g, core, T, topo)
        return
    owner_program(g, core, rank, T, topo)


def helper_program(g, core, T, topo):
    total = 0
    for src in T.cores:
        if topo.chip(src) != topo.chip(core):
            continue
        q = T.rank_of(src)
        for p in [p for u in plan(src, T, topo)[0] for p in u if p["via"] == core]:
            dst = T.cores[p["to"]]
            rid, pid, _ = topo.addr(dst)
            n_in = bits(p["mask"])
            m = topo.mask(core, dst)
            arr = T.sem["arr%d_%d" % (p["half"] or 0, q)]
            a, b, n = column(q, p["half"]), p["at"], p["n"]
            g.wait_ge(T.sem["hcode%d" % p["place"]], n_in)
            g.remote_dma(T.rc[:, a:a + n].bitcast(dt.uint8), T.hc[:, b:b + n].bitcast(dt.uint8), arr, T.sem.sent, pid, rid, m)
            g.wait_ge(T.sem["hplane%d" % p["place"]], n_in)
            g.remote_dma(T.rs[:, a:a + n], T.hs[:, b:b + n], arr, T.sem.sent, pid, rid, m)
            total += 2 * bits(m)
    if total:
        g.wait_ge(T.sem.sent, total)


def arrival(q, r, half, T, topo):
    for i, u in enumerate(plan(T.cores[q], T, topo)[0]):
        for p in u:
            if p["to"] == r and p["half"] in (half, None):
                if p["via"] is None:
                    m, hops = p["mask"], 2
                else:
                    m, hops = topo.mask(p["via"], T.cores[r]), 4
                return i + hops, "arr%d_%d" % (p["half"] or 0, q), 2 * bits(m)


def chain(r, half, T, topo):
    return sorted([0, 1], key=lambda q: 0 if q == r else arrival(q, r, half, T, topo)[0]) + list(range(2, N))


def owner_program(g, core, r, T, topo):
    vec, sca, ten, syn = g.vector, g.scalar, g.tensor, g.sync
    A = AluOpType
    COPY = ActivationFunctionType.Copy
    cnt = {"v": 0, "s": 0, "t": 0}
    seen = {}

    def done(name, ins):
        ins.then_inc(T.sem[name], 1)
        cnt[name] += 1
        return cnt[name]

    def need(queue, me, name, val):
        if val > seen.get((me, name), 0):
            queue.wait_ge(T.sem[name], val)
            seen[(me, name)] = val

    units, _ = plan(core, T, topo)
    others = [d for d in range(N) if d != r]

    for i in range(8):
        (syn if i < 4 else sca).dma_start(T.ids8[16 * i:16 * i + 16, :], T.ids[:, :]).then_inc(T.sem.idl, 16)
    syn.dma_start(T.tb0[:, :], T.tb[:, :]).then_inc(T.sem.tbl, 16)

    n_ones = done("v", vec.memset(T.ones[:, :], 1.0))
    g.wait_ge(T.sem.v, n_ones)
    g.affine_select(T.ez[:, :], T.ones[:, :], [[1, 520]], A.is_equal, 0.0, -4, -4).then_inc(T.sem.ga, 1)

    GROUPS = ((0, 4), (4, N - 1), (N - 1, SLOTS))
    g.wait_ge(T.sem.idl, 128)
    sent = 0
    mine = {d: plan(T.cores[d], T, topo)[1] for d in others}
    for k, (lo_, hi_) in enumerate(GROUPS):
        ids_, dsts, mask, half = [], [], None, k // 2
        for d in sorted(others, key=lambda x: mine[x][(r, half)]):
            s = mine[d][(r, half)]
            if not lo_ <= s < hi_:
                continue
            dst = T.cores[d]
            rid, pid, _ = topo.addr(dst)
            ids_.append(DstId(rid=rid, pnc=pid))
            dsts.append(T.lst[:, LH * s:LH * s + LH])
            m = topo.mask(core, dst)
            mask = m if mask is None else mask & m
        sent += bits(mask)
        g.remote_dma_fused([RemoteDMATransfer(dst_ids=ids_, dma_engine_mask=mask, remote_sem=T.sem["lists%d" % k], srcs=[T.ids8[:, LH * half:LH * half + LH]], dsts=dsts)], local_sem=T.sem.sent)
    each = bits(mask)
    state = {"sent": sent}

    vec.wait_ge(T.sem.ga, 1)
    for b in range(4):
        n_e = done("v", vec.quantize_mx(T.ec[:, 128 * b:128 * b + 128], T.es[:, 128 * b:128 * b + 128], T.ez[:, 4 - b:4 - b + 512]))

    def hashes(src, x, y, off, a, b):
        n = done("v", vec.tensor_scalar(x[:, a:b], src[:, a:b], HA[r], HB[r], A.mult, A.add))
        need(vec, "v", "v", n)
        n = done("v", vec.tensor_scalar(y[:, a:b], x[:, a:b], 3, 4 * (K - 1), A.arith_shift_right, A.bitwise_and))
        need(vec, "v", "v", n)
        return done("v", vec.tensor_copy(off[:, a:b], y[:, a:b]))

    def pick(eng, me, h, off, t, n_off):
        need(eng, me, "v", n_off)
        if t:
            need(eng, me, moved[t][0], moved[t][1])
        o, i = h[:, t:4 * TOK:4], T["tb%d" % t][:, 0:WIN].indirect(off)
        return done(me, sca.activation(o, i, COPY) if me == "s" else vec.tensor_copy(o, i))

    vec.wait_ge(T.sem.idl, 128)
    n_oo = hashes(T.ids8, T.ox, T.oy, T.oo, 0, 16)
    own = {"h": T["h%d" % (N - 1)], "c": T.rc[:, TOK * r:TOK * r + TOK], "p": T.rs[:, TOK * r:TOK * r + TOK]}
    moved = {}
    sca.wait_ge(T.sem.tbl, 16)
    moved[1] = ("s", done("s", sca.activation(T.tb1[:, 0:WIN], T.tb0[:, 1:1 + WIN], COPY)))
    vec.wait_ge(T.sem.tbl, 16)
    for t in (2, 3):
        moved[t] = ("v", done("v", vec.tensor_copy(T["tb%d" % t][:, 0:WIN], T.tb0[:, t:t + WIN])))
    for t in (0, 1):
        own["s"] = pick(sca, "s", own["h"], T.oo[:, 0:16], t, n_oo)
    for t in (2, 3):
        own["v"] = pick(vec, "v", own["h"], T.oo[:, 0:16], t, n_oo)

    def pack(u):
        need(vec, "v", "v", u["v"])
        need(vec, "v", "s", u["s"])
        return done("v", vec.quantize_mx(u["c"], u["p"], u["h"][:, 0:4 * TOK]))

    def pack_and_send(u):
        n = pack(u)
        if "pieces" not in u:
            u["n"] = n
            return
        g.wait_ge(T.sem.v, n)
        codes, planes = [], []
        for p in u["pieces"]:
            a, c, w = column(r, p["half"]), p["col"], p["n"]
            if p["via"] is None:
                dst, oc, op = T.cores[p["to"]], T.rc[:, a:a + w], T.rs[:, a:a + w]
                sc = sp = T.sem["arr%d_%d" % (p["half"] or 0, r)]
            else:
                b = p["at"]
                dst, oc, op = p["via"], T.hc[:, b:b + w], T.hs[:, b:b + w]
                sc, sp = T.sem["hcode%d" % p["place"]], T.sem["hplane%d" % p["place"]]
            rid, pid, _ = topo.addr(dst)
            to = [DstId(rid=rid, pnc=pid)]
            codes.append(RemoteDMATransfer(dst_ids=to, dma_engine_mask=p["mask"], remote_sem=sc, srcs=[u["c"][c:c + w].bitcast(dt.uint8)] if False else [u["qc"][:, c:c + w].bitcast(dt.uint8)], dsts=[oc.bitcast(dt.uint8)]))
            planes.append(RemoteDMATransfer(dst_ids=to, dma_engine_mask=p["mask"], remote_sem=sp, srcs=[u["qs"][:, c:c + w]], dsts=[op]))
            state["sent"] += 2 * bits(p["mask"])
        g.remote_dma_fused(codes, local_sem=T.sem.sent)
        g.remote_dma_fused(planes, local_sem=T.sem.sent)

    n_of = {}

    def listed(ks):
        for k in ks:
            vec.wait_ge(T.sem["lists%d" % k], each * (GROUPS[k][1] - GROUPS[k][0]))
        a, b = GROUPS[ks[0]][0], GROUPS[ks[-1]][1]
        n = hashes(T.lst, T.lx, T.ly, T.lo, LH * a, LH * b)
        for i in range(a, b):
            n_of[i] = n

    listed([0])
    before = own
    for i, pieces in enumerate(units):
        u = {"h": T["h%d" % i], "qc": T["qc%d" % i], "qs": T["qs%d" % i], "c": T["qc%d" % i][:, 0:TOK], "p": T["qs%d" % i][:, 0:TOK], "pieces": pieces}
        s = pieces[0]["slot"]
        off = T.lo[:, LH * s:LH * s + 2 * LH]
        for t in range(SHARE[i]):
            u["s"] = pick(sca, "s", u["h"], off, t, n_of[s + 1])
        for t in range(SHARE[i], 4):
            u["v"] = pick(vec, "v", u["h"], off, t, n_of[s + 1])
            if before is not None:
                pack_and_send(before)
                before = None
        before = u
        if i == 1:
            listed([1, 2])
    pack_and_send(before)

    syn.wait_ge(T.sem.lists0, each * GROUPS[0][1])
    syn.dma_start(T.ws[:, :], T.w[:, :]).then_inc(T.sem.wl, 16)
    vec.wait_ge(T.sem.wl, 16)
    n_w = done("v", vec.quantize_mx(T.wc[:, 0:128 * O], T.wp[:, 0:128 * O], T.ws[:, 0:512 * O]))

    need(ten, "t", "v", n_e)
    waited = {}

    def add(half, k, q):
        if q == r:
            need(ten, "t", "v", own["n"])
        else:
            _, sem, n = arrival(q, r, half, T, topo)
            if sem not in waited:
                ten.wait_ge(T.sem[sem], n)
                waited[sem] = n
        a, n_t = column(q, half), []
        for b in range(4):
            c = 512 * (4 * half + b)
            n_t.append(done("t", ten.matmul_mx(T.ps[:, c:c + H], T.ec[:, 128 * b:128 * b + 128], T.es[:, 128 * b:128 * b + 128],
                                               T.rc[:, a:a + H], T.rs[:, a:a + H], k == 0, k == N - 1)))
        return n_t

    def make_v(half, n_t):
        vt = T["vt%d" % half]
        for b in range(4):
            c = 512 * (4 * half + b)
            o, i = vt[:, b:4 * H:4], T.ps[:, c:c + H]
            if b % 2 == 0:
                need(sca, "s", "t", n_t[b])
                n_s = done("s", sca.activation(o, i, COPY))
            else:
                need(vec, "v", "t", n_t[b])
                n_v = done("v", vec.tensor_copy(o, i))
        need(vec, "v", "v", n_v)
        need(vec, "v", "s", n_s)
        return done("v", vec.quantize_mx(T.vc[:, H * half:H * half + H], T.vs[:, H * half:H * half + H], vt[:, 0:4 * H]))

    def times_w(half, n_q):
        need(ten, "t", "v", n_w)
        need(ten, "t", "v", n_q)
        n = []
        for o in range(O):
            c = 512 * (2 * half + o)
            n.append(done("t", ten.matmul_mx(T.ps[:, c:c + H], T.wc[:, 128 * o:128 * o + 128], T.wp[:, 128 * o:128 * o + 128],
                                             T.vc[:, H * half:H * half + H], T.vs[:, H * half:H * half + H], True, True)))
        return n

    def store(half, n_y):
        y0, y1 = H * half, TOK + H * half
        c = 1024 * half
        need(sca, "s", "t", n_y[0])
        n_s = done("s", sca.activation(T.yo[:, y0:y0 + H], T.ps[:, c:c + H], COPY))
        need(vec, "v", "t", n_y[1])
        n_v = done("v", vec.tensor_copy(T.yo[:, y1:y1 + H], T.ps[:, c + 512:c + 512 + H]))
        if half:
            need(sca, "s", "s", n_s)
            sca.dma_start(T.y[:, y0:y0 + H], T.yo[:, y0:y0 + H]).then_inc(T.sem.yd, 16)
        else:
            need(syn, "y", "s", n_s)
            syn.dma_start(T.y[:, y0:y0 + H], T.yo[:, y0:y0 + H]).then_inc(T.sem.yd, 16)
        need(syn, "y", "v", n_v)
        syn.dma_start(T.y[:, y1:y1 + H], T.yo[:, y1:y1 + H]).then_inc(T.sem.yd, 16)

    for k, q in enumerate(chain(r, 0, T, topo)):
        n_a = add(0, k, q)
    n_q = make_v(0, n_a)
    for k, q in enumerate(chain(r, 1, T, topo)):
        n_b = add(1, k, q)
        if k == 2:
            n_y = times_w(0, n_q)
    store(0, n_y)
    store(1, times_w(1, make_v(1, n_b)))
    syn.wait_ge(T.sem.yd, 64)
    g.wait_ge(T.sem.sent, state["sent"])
